import numpy as np, ml_dtypes
CORES = [2,6,10,14,18,22,26,30]
N = 8
BF = ml_dtypes.bfloat16
F, L, W, S = 16, 256, 16, 16 * 256
def latest(gl):
    i = np.arange(L); return np.max(i - (i * np.asarray(gl).astype(np.int64)[..., None] >> 5), axis=-1)
def shortest(g1, g2):
    return latest(g1) + 1, np.maximum(latest(g2) - (L - 1), 0)
def joined(w, l1, g1, l2, g2):
    return np.concatenate([w, l1, g1, l2, g2], axis=2).astype(np.int32)
def glides(rng):
    return rng.integers(-64, 97, (N, 8, F))
def lags(rng, lo):
    hi = np.maximum(lo, np.minimum(S - 1, L * np.arange(F) + L - 1)); hi = np.where(rng.random(lo.shape) < 0.125, S - 1, hi)
    return rng.integers(lo, hi + 1)
def setup_inputs(rng):
    v = rng.integers(-127, 128, (N, 128, W * L), dtype=np.int8) >> rng.integers(0, 6, (N, 128, 1), dtype=np.int8)
    g1, g2 = glides(rng), glides(rng); m1, m2 = shortest(g1, g2)
    return {"book": v.astype(np.float32).astype(BF), "par": joined(rng.integers(0, W, (N, 8, F)), lags(rng, m1), g1, lags(rng, m2), g2)}
def setup_inputs_near(rng):
    d = setup_inputs(rng); g1, g2 = glides(rng), glides(rng); m1, m2 = shortest(g1, g2)
    l1 = np.minimum(m1 + rng.integers(0, 4, m1.shape) * (rng.random(m1.shape) < 0.5), S - 1); l2 = np.minimum(m2 + rng.integers(0, 4, m2.shape) * (rng.random(m2.shape) < 0.5), S - 1)
    d["par"] = joined(rng.integers(0, W, (N, 8, F)), l1, g1, l2, g2); return d
def setup_inputs_far(rng):
    d = setup_inputs(rng); g = [np.where(rng.random((N, 8, F)) < 0.5, 0, glides(rng)) for k in range(2)]; m = shortest(g[0], g[1]); l = []
    for k in range(2):
        a = L * np.arange(F) + rng.integers(0, L, (N, 8, F)); a = np.where(rng.random(a.shape) < 0.25, S - 1 - rng.integers(0, 2, a.shape), a)
        l.append(np.minimum(np.maximum(a, m[k]), S - 1))
    d["par"] = joined(rng.integers(0, W, (N, 8, F)), l[0], g[0], l[1], g[1]); return d
def setup_inputs_ends(rng):
    d = setup_inputs(rng); e = np.array([-64, -63, -33, -32, -31, -1, 0, 1, 31, 32, 33, 63, 64, 95, 96]); g = [rng.choice(e, (N, 8, F)) for k in range(2)]; m = shortest(g[0], g[1]); l = []
    for k in range(2):
        u = rng.random((N, 8, F)); l.append(np.where(u < 0.25, m[k], np.where(u < 0.375, S - 1, lags(rng, m[k]))))
    d["par"] = joined(rng.choice(np.array([0, W - 1, W >> 1]), (N, 8, F)), l[0], g[0], l[1], g[1]); return d
def setup_inputs_loud(rng):
    d = setup_inputs(rng); v = np.array([-127, -126, 126, 127, -1, 0, 1, 127, -127], np.float32)
    d["book"] = v[rng.integers(0, 9, (N, 128, W * L), dtype=np.int8)].astype(BF); return d
def setup_inputs_spread(rng):
    d = setup_inputs(rng); v = rng.integers(-127, 128, (N, 128, W * L), dtype=np.int8) >> rng.integers(0, 8, (N, 1, W * L), dtype=np.int8)
    d["book"] = (v * (rng.random((N, 1, W * L)) > 0.0625)).astype(np.float32).astype(BF)
    w = d["par"][:, :, :F]; d["par"][:, :, :F] = np.where(rng.random(w.shape) < 0.5, rng.integers(0, W, (N, 8, 1)), w); return d
def check_inputs(d):
    b = d["book"].astype(np.float32); p = d["par"].astype(np.int64); bad = []
    w, l1, g1, l2, g2 = [p[:, :, F * k:F * k + F] for k in range(5)]
    if not ((b == np.floor(b)) & (np.abs(b) <= 127)).all(): bad.append("book")
    if not ((w >= 0) & (w < W)).all(): bad.append("words")
    if not ((l1 >= 0) & (l1 < S) & (l2 >= 0) & (l2 < S)).all(): bad.append("lags")
    if not ((g1 >= -64) & (g1 <= 96) & (g2 >= -64) & (g2 <= 96)).all(): bad.append("glides")
    if not (latest(g1) - l1 < 0).all(): bad.append("own_places")
    if not (latest(g2) - l2 < L).all(): bad.append("lower_places")
    return bad
def reference(book, par):
    w, l1, g1, l2, g2 = [par[:, :, F * k:F * k + F].astype(np.int64) for k in range(5)]
    x = np.zeros((N + 1, 8, 16, S + 1), np.float32); i = np.arange(L)
    for r in range(N):
        b = book[r].astype(np.float32).reshape(8, 16, W, L)
        for k in range(F):
            own = np.maximum(L * k + i - l1[r, :, k, None] - (i * g1[r, :, k, None] >> 5), -1) + 1
            low = np.maximum(L * k + i - l2[r, :, k, None] - (i * g2[r, :, k, None] >> 5), -1) + 1
            for g in range(8):
                v = b[g, :, w[r, g, k]] + x[r + 1, g][:, own[g]] - x[r, g][:, low[g]]
                x[r + 1, g, :, L * k + 1:L * k + L + 1] = np.minimum(np.maximum(v, np.float32(-127)), np.float32(127))
    return {"y": np.ascontiguousarray(x[1:, :, :, 1:]).reshape(N, 128, S)}

@@ -1,0 +1,275 @@
+from concourse.mybir import AluOpType, ActivationFunctionType
+
+F, L, PAD, NR = 16, 256, 16, 8
+S_ALL = F * L
+MODE = "B4"
+RAMP = True
+
+SCRATCH = {
+    "win": ("sbuf", [128, PAD + S_ALL], "bfloat16"),
+    "low": ("sbuf", [128, PAD + S_ALL], "bfloat16"),
+    "bk": ("sbuf", [128, S_ALL], "bfloat16"),
+    "bg": ("sbuf", [128, S_ALL], "bfloat16"),
+    "lg": ("sbuf", [128, S_ALL], "bfloat16"),
+    "cs": ("sbuf", [128, S_ALL], "bfloat16"),
+    "us": ("sbuf", [128, S_ALL], "bfloat16"),
+    "yf": ("sbuf", [128, S_ALL], "float32"),
+    "offb": ("sbuf", [128, 256], "uint16"),
+    "offo": ("sbuf", [128, 256], "uint16"),
+    "offl": ("sbuf", [128, 256], "uint16"),
+    "pi8": ("sbuf", [128, 80], "int32"),
+    "pf8": ("sbuf", [128, 80], "float32"),
+    "ev": ("sbuf", [128, 128], "float32"),
+    "em": ("sbuf", [128, 128], "float32"),
+    "kk": ("sbuf", [128, 16], "float32"),
+    "kf": ("sbuf", [128, 16], "float32"),
+    "pn": ("sbuf", [128, 8], "int32"),
+    "pm": ("sbuf", [128, 8], "int32"),
+    "pmf": ("sbuf", [128, 8], "float32"),
+    "c16": ("sbuf", [128, 16], "float32"),
+    "i16": ("sbuf", [128, 16], "float32"),
+    "idv": ("sbuf", [128, 128], "float32"),
+    "ident": ("sbuf", [128, 128], "bfloat16"),
+    "ps": ("psum", [128, S_ALL], "float32"),
+}
+SEMAPHORES = (["par", "bookin", "ka", "kb", "vs", "vid", "pb", "pad", "t0", "t1", "a0", "a1", "b0", "cc", "sent", "st"]
+              + ["arr%d" % k for k in range(F)] + ["lg%d" % k for k in range(F)] + ["bg%d" % k for k in range(F)]
+              + ["ix%d" % k for k in range(F)] + ["cv%d" % k for k in range(F)] + ["pe%d" % k for k in range(8)])
+
+
+def store_plan(rank):
+    if rank == NR - 1:
+        return [(k, k + 1, False) for k in range(0, 14, 2)] + [(14, 14, False), (15, 15, False)]
+    if rank == NR - 2:
+        return [(0, 2, False), (3, 5, False), (6, 8, False), (9, 11, False), (12, 15, True)]
+    return [(0, 15, True)]
+
+
+def rank_program(g, core, T, topo):
+    rank = T.rank_of(core)
+    if rank is None:
+        return
+    A, Fn = AluOpType, ActivationFunctionType
+    V, S, PE, Q = g.vector, g.scalar, g.tensor, g.sync
+    first, last = rank == 0, rank == NR - 1
+    neg = (NR - 1 - rank) % 2 == 1
+    wop = A.subtract if neg else A.add
+    tot, seen = {}, {}
+
+    def inc(ins, name, n=1):
+        ins.then_inc(T.sem[name], n)
+        tot[name] = tot.get(name, 0) + n
+
+    def wait(q, name, val=None):
+        v = tot[name] if val is None else val
+        q.wait_ge(T.sem[name], v)
+        seen[name] = max(seen.get(name, 0), v)
+
+    def fr(buf, f, a=0, b=L, pad=0):
+        return buf[:, pad + L * f + a:pad + L * f + b]
+
+    def lst(buf, f, a=0, b=L):
+        return buf[:, 16 * f + a // 16:16 * f + b // 16]
+
+    def engines_of(src, dst, f):
+        es = topo.engines(src, dst)
+        if RAMP and f == 0 and topo.chip(src) == topo.chip(dst):
+            es = es[::2]
+        return es
+
+    if not first:
+        for f in range(F):
+            tot["arr%d" % f] = len(engines_of(T.cores[rank - 1], core, f))
+
+    inc(Q.dma_start(T.pi8[0:8, :], T.par[:, :]), "par", 16)
+    inc(Q.dma_start(T.bk[:, :], T.book[:, :]), "bookin", 16)
+
+    inc(g.iota(T.ev[0:8, :], [[1, 8], [0, 16]], 0, -1, allow_small_or_imprecise_dtypes=True), "ka")
+    inc(g.iota(T.kk[0:8, :], [[L, 16]], PAD, 0, allow_small_or_imprecise_dtypes=True), "ka")
+    inc(g.iota(T.pn[:, 0:1], [[1, 1]], 0, 1), "ka")
+    inc(g.iota(T.c16[:, :], [[16, 16]], 0, 0, allow_small_or_imprecise_dtypes=True), "ka")
+    use_pe = MODE == "B4" and not first
+    if use_pe:
+        inc(g.iota(T.idv[:, :], [[-1, 128]], 0, 1, allow_small_or_imprecise_dtypes=True), "kb")
+    inc(V.memset(T.win[:, 0:PAD], 0.0), "pad")
+    if not first:
+        inc(V.memset(T.low[:, 0:PAD], 0.0), "pad")
+    wait(V, "ka")
+    inc(V.tensor_scalar(T.pm[:, 0:1], T.pn[:, 0:1], 15, None, A.bitwise_and), "vs")
+    inc(V.tensor_scalar(T.em[0:8, :], T.ev[0:8, :], 0.0, None, A.is_equal), "vs")
+    inc(V.tensor_scalar(T.kf[0:8, :], T.kk[0:8, :], 15.5 / 32, None, A.add), "vs")
+    wait(V, "vs")
+    inc(V.tensor_copy(T.pmf[:, 0:1], T.pm[:, 0:1]), "vs")
+    wait(V, "vs")
+    inc(V.tensor_scalar(T.i16[:, :], T.c16[:, :], T.pmf[:, 0:1], None, A.add), "vs")
+    if use_pe:
+        wait(V, "kb")
+        inc(V.tensor_scalar(T.ident[:, :], T.idv[:, :], 0.0, None, A.is_equal), "vid")
+
+    wait(V, "par")
+    inc(V.tensor_scalar(T.pf8[0:8, 0:16], T.pi8[0:8, 0:16], float(L), None, A.mult), "vs")
+    ncol = 48 if first else 80
+    for c0 in range(16, ncol, 32):
+        inc(V.tensor_tensor(T.pf8[0:8, c0:c0 + 16], T.kf[0:8, :], T.pi8[0:8, c0:c0 + 16], A.subtract), "vs")
+        inc(V.tensor_scalar(T.pf8[0:8, c0 + 16:c0 + 32], T.pi8[0:8, c0 + 16:c0 + 32], -1.0 / 32, 1.0, A.mult, A.add), "vs")
+    wait(PE, "vs")
+    inc(PE.matmul(T.ps[:, 0:ncol], T.em[0:8, :], T.pf8[0:8, 0:ncol], True, True), "pb")
+    wait(V, "vs")
+    wait(V, "pb")
+
+    def word_list(f, sem):
+        inc(V.tensor_scalar(lst(T.offb, f), T.i16[:, :], T.ps[:, f:f + 1], None, A.add), sem)
+
+    def place_list(buf, c0, f, sem):
+        inc(V.tensor_scalar(lst(buf, f), T.i16[:, :], T.ps[:, c0 + 16 + f:c0 + 17 + f], T.ps[:, c0 + f:c0 + f + 1],
+                            A.mult, A.add), sem)
+
+    halves = [(0, L // 2), (L // 2, L)]
+
+    def clip(f, a, b, n):
+        out = fr(T.yf, f, a, b) if (last and f == F - 1) else fr(T.win, f, a, b, PAD)
+        inc(V.tensor_scalar(out, fr(T.us, f, a, b), -127.0, 127.0, A.max, A.min), "cc", n)
+
+    def own(f, a, b):
+        return T.win[:, 0:PAD + L * f].indirect(lst(T.offo, f, a, b))
+
+    def lower(f, a, b):
+        return T.low[:, 0:PAD + L * (f + 1)].indirect(lst(T.offl, f, a, b))
+
+    def words(f0, f1, a=0, b=L):
+        return T.bk[:, :].indirect(T.offb[:, 16 * f0 + a // 16:16 * f1 + b // 16])
+
+    plan = store_plan(rank)
+    batch_of = {}
+    for j, (f0, f1, late) in enumerate(plan):
+        for f in range(f0, f1 + 1):
+            batch_of[f] = j
+    nconv = F - 1 if last else F
+
+    def convert(f0, f1):
+        wait(S, "cc", 2 * (f1 + 1))
+        inc(S.activation(T.yf[:, L * f0:L * (f1 + 1)], T.win[:, PAD + L * f0:PAD + L * (f1 + 1)], Fn.Copy,
+                         scale=-1.0 if neg else 1.0), "cv%d" % batch_of[f0])
+
+    if first:
+        ahead = 3
+        for f in range(ahead + 1):
+            word_list(f, "ix%d" % f)
+            if f:
+                place_list(T.offo, 16, f, "ix%d" % f)
+        for q in (V, S):
+            wait(q, "ix0")
+            wait(q, "bookin")
+        inc(V.tensor_scalar(fr(T.win, 0, 0, L // 2, PAD), words(0, 0, 0, L // 2), -1.0 if neg else 1.0, None, A.mult), "cc")
+        inc(S.activation(fr(T.win, 0, L // 2, L, PAD), words(0, 0, L // 2, L), Fn.Copy, scale=-1.0 if neg else 1.0), "cc")
+        wait(V, "pad")
+        for f in range(1, F):
+            if f + ahead < F:
+                word_list(f + ahead, "ix%d" % (f + ahead))
+                place_list(T.offo, 16, f + ahead, "ix%d" % (f + ahead))
+            wait(S, "ix%d" % f)
+            inc(S.activation(fr(T.bg, f), words(f, f), Fn.Copy), "bg%d" % f)
+            wait(V, "ix%d" % f)
+            wait(V, "bg%d" % f)
+            wait(V, "cc")
+            inc(V.tensor_tensor(fr(T.us, f), own(f, 0, L), fr(T.bg, f), wop), "a0")
+            wait(V, "a0")
+            clip(f, 0, L, 2)
+        for f0 in range(0, F, 4):
+            convert(f0, f0 + 3)
+    else:
+        for f in range(F):
+            word_list(f, "ix0")
+        for f in range(F):
+            place_list(T.offl, 48, f, "ix1")
+        for f in range(1, F):
+            place_list(T.offo, 16, f, "ix1")
+
+        def word_pair(j):
+            inc(S.activation(T.bg[:, 2 * L * j:2 * L * (j + 1)], words(2 * j, 2 * j + 1), Fn.Copy), "bg%d" % j)
+            if use_pe:
+                wait(PE, "bg%d" % j)
+                c0 = L if j == 0 else 2 * L * j
+                inc(PE.matmul(T.ps[:, c0:2 * L * (j + 1)], T.ident[:, :], T.bg[:, c0:2 * L * (j + 1)], True, True), "pe%d" % j)
+
+        if use_pe:
+            wait(PE, "vid")
+            wait(PE, "ix0")
+            wait(PE, "ix1")
+        wait(S, "ix0")
+        wait(S, "bookin")
+        early = 4 if (rank == 1 and use_pe) else 8
+        for j in range(early):
+            word_pair(j)
+        if use_pe:
+            wait(S, "ix1")
+            wait(S, "pad")
+            wait(S, "arr0")
+        todo, nxt = list(range(early, 8)), 0
+        for f in range(1, F):
+            if use_pe:
+                wait(S, "arr%d" % f)
+                inc(S.activation(fr(T.lg, f), lower(f, 0, L), Fn.Copy), "lg%d" % f)
+            if todo:
+                if f % 2 == 1:
+                    word_pair(todo.pop(0))
+                continue
+            if nxt <= f - 2:
+                hi = nxt + 1 if (nxt + 1 <= f - 2 and batch_of[nxt + 1] == batch_of[nxt]) else nxt
+                convert(nxt, hi)
+                nxt = hi + 1
+        while nxt < nconv:
+            convert(nxt, nxt)
+            nxt += 1
+
+        wait(V, "ix1")
+        wait(V, "pad")
+        wait(V, "bg0")
+        wait(V, "arr0")
+        inc(V.tensor_tensor(fr(T.us, 0), lower(0, 0, L), fr(T.bg, 0), wop), "b0")
+        wait(V, "b0")
+        clip(0, 0, L, 2)
+        for f in range(1, F):
+            if MODE == "B4":
+                if f == 1 or f % 2 == 0:
+                    wait(V, "pe%d" % (f // 2))
+                wait(V, "lg%d" % f)
+                for h, (a, b) in enumerate(halves):
+                    inc(V.tensor_tensor(fr(T.cs, f, a, b), fr(T.lg, f, a, b), fr(T.ps, f, a, b), wop), "t%d" % h)
+            else:
+                if f % 2 == 0:
+                    wait(V, "bg%d" % (f // 2))
+                wait(V, "arr%d" % f)
+                for h, (a, b) in enumerate(halves):
+                    inc(V.tensor_tensor(fr(T.cs, f, a, b), lower(f, a, b), fr(T.bg, f, a, b), wop), "t%d" % h)
+            wait(V, "cc", 2 * f)
+            for h, (a, b) in enumerate(halves):
+                wait(V, "t%d" % h)
+                inc(V.tensor_tensor(fr(T.us, f, a, b), own(f, a, b), fr(T.cs, f, a, b), A.add), "a%d" % h)
+            for h, (a, b) in enumerate(halves):
+                wait(V, "a%d" % h)
+                clip(f, a, b, 1)
+
+    if not last:
+        dst = T.cores[rank + 1]
+        rid, pid, _ = topo.addr(dst)
+        tot["sent"] = 0
+        for f in range(F):
+            es = engines_of(core, dst, f)
+            wait(g, "cc", 2 * (f + 1))
+            g.remote_dma(fr(T.low, f, 0, L, PAD), fr(T.win, f, 0, L, PAD), T.sem["arr%d" % f], T.sem["sent"], pid, rid,
+                         sum(1 << e for e in es))
+            tot["sent"] += len(es)
+
+    for j, (f0, f1, late) in enumerate(plan):
+        if last and f1 == F - 1:
+            wait(Q, "cc", 2 * F)
+        else:
+            wait(Q, "cv%d" % j)
+        if late:
+            wait(Q, "sent")
+        inc(Q.dma_start(T.y[:, L * f0:L * (f1 + 1)], T.yf[:, L * f0:L * (f1 + 1)]), "st", 16)
+    for name in tot:
+        if name != "st" and seen.get(name, 0) < tot[name]:
+            wait(g, name)
+    wait(Q, "st")

@@ -2,8 +2,8 @@ from concourse.mybir import AluOpType, ActivationFunctionType
 
 F, L, PAD, NR = 16, 256, 16, 8
 S_ALL = F * L
-MODE = "B4"
-RAMP = True
+H = L // 2
+HALVES = [(0, H), (H, L)]
 
 SCRATCH = {
     "win": ("sbuf", [128, PAD + S_ALL], "bfloat16"),
@@ -32,16 +32,18 @@ SCRATCH = {
     "ident": ("sbuf", [128, 128], "bfloat16"),
     "ps": ("psum", [128, S_ALL], "float32"),
 }
-SEMAPHORES = (["par", "bookin", "ka", "kb", "vs", "vid", "pb", "pad", "t0", "t1", "a0", "a1", "b0", "cc", "sent", "st"]
-              + ["arr%d" % k for k in range(F)] + ["lg%d" % k for k in range(F)] + ["bg%d" % k for k in range(F)]
-              + ["ix%d" % k for k in range(F)] + ["cv%d" % k for k in range(F)] + ["pe%d" % k for k in range(8)])
+SEMAPHORES = (["par", "bookin", "ka", "kb", "vs", "vid", "pb", "pad", "wl", "ll", "ol", "t0", "t1", "a0", "a1", "cc",
+               "lg", "pe", "sent", "st"]
+              + ["arr%d" % k for k in range(F)] + ["bg%d" % k for k in range(F)] + ["cv%d" % k for k in range(F)])
 
 
 def store_plan(rank):
     if rank == NR - 1:
-        return [(k, k + 1, False) for k in range(0, 14, 2)] + [(14, 14, False), (15, 15, False)]
+        return [(k, k + 1, False) for k in range(0, 14, 2)] + [(14, 14, False)]
     if rank == NR - 2:
-        return [(0, 2, False), (3, 5, False), (6, 8, False), (9, 11, False), (12, 15, True)]
+        return [(k, k, False) for k in range(13)] + [(13, 15, True)]
+    if rank == 1:
+        return [(k, k + 3, True) for k in range(0, F, 4)]
     return [(0, 15, True)]
 
 
@@ -52,8 +54,7 @@ def rank_program(g, core, T, topo):
     A, Fn = AluOpType, ActivationFunctionType
     V, S, PE, Q = g.vector, g.scalar, g.tensor, g.sync
     first, last = rank == 0, rank == NR - 1
-    neg = (NR - 1 - rank) % 2 == 1
-    wop = A.subtract if neg else A.add
+    sgn = -1.0 if (NR - 1 - rank) % 2 == 1 else 1.0
     tot, seen = {}, {}
 
     def inc(ins, name, n=1):
@@ -68,18 +69,15 @@ def rank_program(g, core, T, topo):
     def fr(buf, f, a=0, b=L, pad=0):
         return buf[:, pad + L * f + a:pad + L * f + b]
 
+    def frs(buf, f0, f1):
+        return buf[:, L * f0:L * (f1 + 1)]
+
     def lst(buf, f, a=0, b=L):
         return buf[:, 16 * f + a // 16:16 * f + b // 16]
 
-    def engines_of(src, dst, f):
-        es = topo.engines(src, dst)
-        if RAMP and f == 0 and topo.chip(src) == topo.chip(dst):
-            es = es[::2]
-        return es
-
     if not first:
         for f in range(F):
-            tot["arr%d" % f] = len(engines_of(T.cores[rank - 1], core, f))
+            tot["arr%d" % f] = len(topo.engines(T.cores[rank - 1], core))
 
     inc(Q.dma_start(T.pi8[0:8, :], T.par[:, :]), "par", 16)
     inc(Q.dma_start(T.bk[:, :], T.book[:, :]), "bookin", 16)
@@ -88,8 +86,7 @@ def rank_program(g, core, T, topo):
     inc(g.iota(T.kk[0:8, :], [[L, 16]], PAD, 0, allow_small_or_imprecise_dtypes=True), "ka")
     inc(g.iota(T.pn[:, 0:1], [[1, 1]], 0, 1), "ka")
     inc(g.iota(T.c16[:, :], [[16, 16]], 0, 0, allow_small_or_imprecise_dtypes=True), "ka")
-    use_pe = MODE == "B4" and not first
-    if use_pe:
+    if not first:
         inc(g.iota(T.idv[:, :], [[-1, 128]], 0, 1, allow_small_or_imprecise_dtypes=True), "kb")
     inc(V.memset(T.win[:, 0:PAD], 0.0), "pad")
     if not first:
@@ -102,7 +99,7 @@ def rank_program(g, core, T, topo):
     inc(V.tensor_copy(T.pmf[:, 0:1], T.pm[:, 0:1]), "vs")
     wait(V, "vs")
     inc(V.tensor_scalar(T.i16[:, :], T.c16[:, :], T.pmf[:, 0:1], None, A.add), "vs")
-    if use_pe:
+    if not first:
         wait(V, "kb")
         inc(V.tensor_scalar(T.ident[:, :], T.idv[:, :], 0.0, None, A.is_equal), "vid")
 
@@ -117,158 +114,185 @@ def rank_program(g, core, T, topo):
     wait(V, "vs")
     wait(V, "pb")
 
-    def word_list(f, sem):
-        inc(V.tensor_scalar(lst(T.offb, f), T.i16[:, :], T.ps[:, f:f + 1], None, A.add), sem)
+    def word_list(f):
+        inc(V.tensor_scalar(lst(T.offb, f), T.i16[:, :], T.ps[:, f:f + 1], None, A.add), "wl")
 
     def place_list(buf, c0, f, sem):
         inc(V.tensor_scalar(lst(buf, f), T.i16[:, :], T.ps[:, c0 + 16 + f:c0 + 17 + f], T.ps[:, c0 + f:c0 + f + 1],
                             A.mult, A.add), sem)
 
-    halves = [(0, L // 2), (L // 2, L)]
+    def own_list(f):
+        place_list(T.offo, 16, f, "ol")
 
-    def clip(f, a, b, n):
-        out = fr(T.yf, f, a, b) if (last and f == F - 1) else fr(T.win, f, a, b, PAD)
-        inc(V.tensor_scalar(out, fr(T.us, f, a, b), -127.0, 127.0, A.max, A.min), "cc", n)
-
-    def own(f, a, b):
+    def own(f, a=0, b=L):
         return T.win[:, 0:PAD + L * f].indirect(lst(T.offo, f, a, b))
 
-    def lower(f, a, b):
+    def lower(f, a=0, b=L):
         return T.low[:, 0:PAD + L * (f + 1)].indirect(lst(T.offl, f, a, b))
 
-    def words(f0, f1, a=0, b=L):
-        return T.bk[:, :].indirect(T.offb[:, 16 * f0 + a // 16:16 * f1 + b // 16])
+    def words(q, out, offs, sem):
+        src = T.bk[:, :].indirect(offs)
+        if q is V:
+            inc(V.tensor_scalar(out, src, sgn, None, A.mult), sem)
+        else:
+            inc(S.activation(out, src, Fn.Copy, scale=sgn), sem)
+
+    def word_run(q, f0, f1):
+        words(q, frs(T.bg, f0, f1), T.offb[:, 16 * f0:16 * (f1 + 1)], "bg%d" % f0)
+
+    def clip(f, a, b, n, wide=False):
+        out = fr(T.yf, f, a, b) if wide else fr(T.win, f, a, b, PAD)
+        inc(V.tensor_scalar(out, fr(T.us, f, a, b), -127.0, 127.0, A.max, A.min), "cc", n)
 
     plan = store_plan(rank)
     batch_of = {}
     for j, (f0, f1, late) in enumerate(plan):
         for f in range(f0, f1 + 1):
             batch_of[f] = j
-    nconv = F - 1 if last else F
 
-    def convert(f0, f1):
-        wait(S, "cc", 2 * (f1 + 1))
-        inc(S.activation(T.yf[:, L * f0:L * (f1 + 1)], T.win[:, PAD + L * f0:PAD + L * (f1 + 1)], Fn.Copy,
-                         scale=-1.0 if neg else 1.0), "cv%d" % batch_of[f0])
+    def convert(q, f0, f1):
+        sem = "cv%d" % batch_of[f0]
+        src = T.win[:, PAD + L * f0:PAD + L * (f1 + 1)]
+        wait(q, "cc", 2 * (f1 + 1))
+        if q is V:
+            inc(V.tensor_scalar(frs(T.yf, f0, f1), src, sgn, None, A.mult), sem)
+        else:
+            inc(S.activation(frs(T.yf, f0, f1), src, Fn.Copy, scale=sgn), sem)
 
     if first:
-        ahead = 3
-        for f in range(ahead + 1):
-            word_list(f, "ix%d" % f)
-            if f:
-                place_list(T.offo, 16, f, "ix%d" % f)
-        for q in (V, S):
-            wait(q, "ix0")
+        for f in range(4):
+            word_list(f)
+        for f in range(1, 3):
+            own_list(f)
+        for q, (a, b) in zip((V, S), HALVES):
+            wait(q, "wl", 2)
             wait(q, "bookin")
-        inc(V.tensor_scalar(fr(T.win, 0, 0, L // 2, PAD), words(0, 0, 0, L // 2), -1.0 if neg else 1.0, None, A.mult), "cc")
-        inc(S.activation(fr(T.win, 0, L // 2, L, PAD), words(0, 0, L // 2, L), Fn.Copy, scale=-1.0 if neg else 1.0), "cc")
+            words(q, fr(T.win, 0, a, b, PAD), lst(T.offb, 0, a, b), "cc")
+            words(q, fr(T.bg, 1, a, b), lst(T.offb, 1, a, b), "bg1")
         wait(V, "pad")
+        for f in range(2, F):
+            wait(S, "wl", f + 1)
+            word_run(S, f, f)
         for f in range(1, F):
-            if f + ahead < F:
-                word_list(f + ahead, "ix%d" % (f + ahead))
-                place_list(T.offo, 16, f + ahead, "ix%d" % (f + ahead))
-            wait(S, "ix%d" % f)
-            inc(S.activation(fr(T.bg, f), words(f, f), Fn.Copy), "bg%d" % f)
-            wait(V, "ix%d" % f)
+            wait(V, "ol", f)
             wait(V, "bg%d" % f)
-            wait(V, "cc")
-            inc(V.tensor_tensor(fr(T.us, f), own(f, 0, L), fr(T.bg, f), wop), "a0")
+            wait(V, "cc", 2 * f)
+            inc(V.tensor_tensor(fr(T.us, f), own(f), fr(T.bg, f), A.add), "a0")
+            if f + 2 < F:
+                own_list(f + 2)
             wait(V, "a0")
             clip(f, 0, L, 2)
+            if f + 3 < F:
+                word_list(f + 3)
         for f0 in range(0, F, 4):
-            convert(f0, f0 + 3)
+            convert(S, f0, f0 + 3)
     else:
         for f in range(F):
-            word_list(f, "ix0")
+            word_list(f)
         for f in range(F):
-            place_list(T.offl, 48, f, "ix1")
+            place_list(T.offl, 48, f, "ll")
         for f in range(1, F):
-            place_list(T.offo, 16, f, "ix1")
+            own_list(f)
 
-        def word_pair(j):
-            inc(S.activation(T.bg[:, 2 * L * j:2 * L * (j + 1)], words(2 * j, 2 * j + 1), Fn.Copy), "bg%d" % j)
-            if use_pe:
-                wait(PE, "bg%d" % j)
-                c0 = L if j == 0 else 2 * L * j
-                inc(PE.matmul(T.ps[:, c0:2 * L * (j + 1)], T.ident[:, :], T.bg[:, c0:2 * L * (j + 1)], True, True), "pe%d" % j)
+        for q in (V, S):
+            wait(q, "wl")
+            wait(q, "bookin")
+        word_run(V, F - 1 if rank == 1 else 12, F - 1)
+        for f0, f1 in [(0, 1), (2, 5)] + ([] if rank == 1 else [(6, 11)]):
+            word_run(S, f0, f1)
+        between = dict(zip((1, 2, 4, 5, 7, 8, 10, 11, 12), range(6, 15)))
 
-        if use_pe:
-            wait(PE, "vid")
-            wait(PE, "ix0")
-            wait(PE, "ix1")
-        wait(S, "ix0")
-        wait(S, "bookin")
-        early = 4 if (rank == 1 and use_pe) else 8
-        for j in range(early):
-            word_pair(j)
-        if use_pe:
-            wait(S, "ix1")
-            wait(S, "pad")
-            wait(S, "arr0")
-        todo, nxt = list(range(early, 8)), 0
+        wait(S, "ll")
+        wait(S, "pad")
+        wait(S, "arr0")
         for f in range(1, F):
-            if use_pe:
-                wait(S, "arr%d" % f)
-                inc(S.activation(fr(T.lg, f), lower(f, 0, L), Fn.Copy), "lg%d" % f)
-            if todo:
-                if f % 2 == 1:
-                    word_pair(todo.pop(0))
-                continue
-            if nxt <= f - 2:
-                hi = nxt + 1 if (nxt + 1 <= f - 2 and batch_of[nxt + 1] == batch_of[nxt]) else nxt
-                convert(nxt, hi)
-                nxt = hi + 1
-        while nxt < nconv:
-            convert(nxt, nxt)
-            nxt += 1
+            wait(S, "arr%d" % f)
+            for a, b in HALVES:
+                inc(S.activation(fr(T.lg, f, a, b), lower(f, a, b), Fn.Copy), "lg")
+            if rank == 1:
+                if f in between:
+                    word_run(S, between[f], between[f])
+            elif f >= 2:
+                convert(S, f - 2, f - 2)
+        if last:
+            for h, (a, b) in enumerate(HALVES):
+                wait(S, "cc", 2 * F - 3 + h)
+                inc(S.activation(fr(T.yf, F - 2, a, b), fr(T.win, F - 2, a, b, PAD), Fn.Copy), "cv%d" % batch_of[F - 2])
+        elif rank > 1:
+            for f in range(F - 2, F):
+                convert(S, f, f)
 
-        wait(V, "ix1")
-        wait(V, "pad")
-        wait(V, "bg0")
-        wait(V, "arr0")
-        inc(V.tensor_tensor(fr(T.us, 0), lower(0, 0, L), fr(T.bg, 0), wop), "b0")
-        wait(V, "b0")
-        clip(0, 0, L, 2)
+        for name in ("vid", "wl", "ll", "ol"):
+            wait(PE, name)
+        def psw(f, a=0, b=L):
+            return fr(T.ps, 2 * (f % 8) + 1 - f // 8, a, b)
+
+        wait(PE, "bg0")
         for f in range(1, F):
-            if MODE == "B4":
-                if f == 1 or f % 2 == 0:
-                    wait(V, "pe%d" % (f // 2))
-                wait(V, "lg%d" % f)
-                for h, (a, b) in enumerate(halves):
-                    inc(V.tensor_tensor(fr(T.cs, f, a, b), fr(T.lg, f, a, b), fr(T.ps, f, a, b), wop), "t%d" % h)
-            else:
-                if f % 2 == 0:
-                    wait(V, "bg%d" % (f // 2))
-                wait(V, "arr%d" % f)
-                for h, (a, b) in enumerate(halves):
-                    inc(V.tensor_tensor(fr(T.cs, f, a, b), lower(f, a, b), fr(T.bg, f, a, b), wop), "t%d" % h)
+            if "bg%d" % f in tot:
+                wait(PE, "bg%d" % f)
+            if f > 8:
+                wait(PE, "t0", f - 8)
+                wait(PE, "t1", f - 8)
+            inc(PE.matmul(psw(f), T.ident[:, :], fr(T.bg, f), True, True), "pe")
+
+        def add(f, h):
+            a, b = HALVES[h]
+            if h == 0:
+                wait(V, "pe", f)
+            wait(V, "lg", 2 * (f - 1) + h + 1)
+            inc(V.tensor_tensor(fr(T.cs, f, a, b), fr(T.lg, f, a, b), psw(f, a, b), A.add), "t%d" % h)
+
+        for name in ("ll", "ol", "pad", "bg0", "arr0"):
+            wait(V, name)
+        for h, (a, b) in enumerate(HALVES):
+            inc(V.tensor_tensor(fr(T.us, 0, a, b), lower(0, a, b), fr(T.bg, 0, a, b), A.add), "a%d" % h)
+        for h, (a, b) in enumerate(HALVES):
+            wait(V, "a%d" % h)
+            clip(0, a, b, 1)
+        add(1, 0)
+        add(1, 1)
+        for f in range(1, F):
             wait(V, "cc", 2 * f)
-            for h, (a, b) in enumerate(halves):
+            for h, (a, b) in enumerate(HALVES):
                 wait(V, "t%d" % h)
                 inc(V.tensor_tensor(fr(T.us, f, a, b), own(f, a, b), fr(T.cs, f, a, b), A.add), "a%d" % h)
-            for h, (a, b) in enumerate(halves):
+            for h, (a, b) in enumerate(HALVES):
+                if h == 1 and f + 1 < F:
+                    add(f + 1, 0)
                 wait(V, "a%d" % h)
-                clip(f, a, b, 1)
+                clip(f, a, b, 1, last and f == F - 1)
+            if f + 1 < F:
+                add(f + 1, 1)
+        if rank == 1:
+            for f0 in range(0, F, 4):
+                convert(V, f0, f0 + 1)
+                convert(S, f0 + 2, f0 + 3)
 
     if not last:
         dst = T.cores[rank + 1]
         rid, pid, _ = topo.addr(dst)
         tot["sent"] = 0
-        for f in range(F):
-            es = engines_of(core, dst, f)
-            wait(g, "cc", 2 * (f + 1))
-            g.remote_dma(fr(T.low, f, 0, L, PAD), fr(T.win, f, 0, L, PAD), T.sem["arr%d" % f], T.sem["sent"], pid, rid,
-                         sum(1 << e for e in es))
-            tot["sent"] += len(es)
+        es = topo.engines(core, dst)
+        pieces = [(0, a, b, 2 if first else h + 1, es[h::2]) for h, (a, b) in enumerate(HALVES)]
+        for f, a, b, done, use in pieces + [(f, 0, L, 2 * (f + 1), es) for f in range(1, F)]:
+            wait(g, "cc", done)
+            g.remote_dma(fr(T.low, f, a, b, PAD), fr(T.win, f, a, b, PAD), T.sem["arr%d" % f], T.sem["sent"], pid, rid,
+                         sum(1 << e for e in use))
+            tot["sent"] += len(use)
 
     for j, (f0, f1, late) in enumerate(plan):
-        if last and f1 == F - 1:
-            wait(Q, "cc", 2 * F)
-        else:
-            wait(Q, "cv%d" % j)
+        wait(Q, "cv%d" % j)
         if late:
             wait(Q, "sent")
-        inc(Q.dma_start(T.y[:, L * f0:L * (f1 + 1)], T.yf[:, L * f0:L * (f1 + 1)]), "st", 16)
+        c0, c1 = L * f0, L * (f1 + 1)
+        if rank == NR - 2:
+            c0, c1 = 192 * j, S_ALL if late else 192 * (j + 1)
+        inc(Q.dma_start(T.y[:, c0:c1], T.yf[:, c0:c1]), "st", 16)
+    if last:
+        for h, q in enumerate((Q, S)):
+            wait(q, "cc", 2 * F - 1 + h)
+            inc(q.dma_start(fr(T.y, F - 1, H * h, H * (h + 1)), fr(T.yf, F - 1, H * h, H * (h + 1))), "st", 16)
     for name in tot:
         if name != "st" and seen.get(name, 0) < tot[name]:
             wait(g, name)

from concourse.mybir import AluOpType, ActivationFunctionType

F, L, PAD, NR = 16, 256, 16, 8
S_ALL = F * L
H = L // 2
HALVES = [(0, H), (H, L)]

SCRATCH = {
    "win": ("sbuf", [128, PAD + S_ALL], "bfloat16"),
    "low": ("sbuf", [128, PAD + S_ALL], "bfloat16"),
    "bk": ("sbuf", [128, S_ALL], "bfloat16"),
    "bg": ("sbuf", [128, S_ALL], "bfloat16"),
    "lg": ("sbuf", [128, S_ALL], "bfloat16"),
    "cs": ("sbuf", [128, S_ALL], "bfloat16"),
    "us": ("sbuf", [128, S_ALL], "bfloat16"),
    "yf": ("sbuf", [128, S_ALL], "float32"),
    "offb": ("sbuf", [128, 256], "uint16"),
    "offo": ("sbuf", [128, 256], "uint16"),
    "offl": ("sbuf", [128, 256], "uint16"),
    "pi8": ("sbuf", [128, 80], "int32"),
    "pf8": ("sbuf", [128, 80], "float32"),
    "ev": ("sbuf", [128, 128], "float32"),
    "em": ("sbuf", [128, 128], "float32"),
    "kk": ("sbuf", [128, 16], "float32"),
    "kf": ("sbuf", [128, 16], "float32"),
    "pn": ("sbuf", [128, 8], "int32"),
    "pm": ("sbuf", [128, 8], "int32"),
    "pmf": ("sbuf", [128, 8], "float32"),
    "c16": ("sbuf", [128, 16], "float32"),
    "i16": ("sbuf", [128, 16], "float32"),
    "idv": ("sbuf", [128, 128], "float32"),
    "ident": ("sbuf", [128, 128], "bfloat16"),
    "ps": ("psum", [128, S_ALL], "float32"),
}
SEMAPHORES = (["par", "bookin", "ka", "kb", "vs", "vid", "pb", "pad", "wl", "ll", "ol", "t0", "t1", "a0", "a1", "cc",
               "lg", "pe", "sent", "st"]
              + ["arr%d" % k for k in range(F)] + ["bg%d" % k for k in range(F)] + ["cv%d" % k for k in range(F)])


def store_plan(rank):
    if rank == NR - 1:
        return [(k, k + 1, False) for k in range(0, 14, 2)] + [(14, 14, False)]
    if rank == NR - 2:
        return [(k, k, False) for k in range(13)] + [(13, 15, True)]
    if rank == 1:
        return [(k, k + 3, True) for k in range(0, F, 4)]
    return [(0, 15, True)]


def rank_program(g, core, T, topo):
    rank = T.rank_of(core)
    if rank is None:
        return
    A, Fn = AluOpType, ActivationFunctionType
    V, S, PE, Q = g.vector, g.scalar, g.tensor, g.sync
    first, last = rank == 0, rank == NR - 1
    sgn = -1.0 if (NR - 1 - rank) % 2 == 1 else 1.0
    tot, seen = {}, {}

    def inc(ins, name, n=1):
        ins.then_inc(T.sem[name], n)
        tot[name] = tot.get(name, 0) + n

    def wait(q, name, val=None):
        v = tot[name] if val is None else val
        q.wait_ge(T.sem[name], v)
        seen[name] = max(seen.get(name, 0), v)

    def fr(buf, f, a=0, b=L, pad=0):
        return buf[:, pad + L * f + a:pad + L * f + b]

    def frs(buf, f0, f1):
        return buf[:, L * f0:L * (f1 + 1)]

    def lst(buf, f, a=0, b=L):
        return buf[:, 16 * f + a // 16:16 * f + b // 16]

    if not first:
        for f in range(F):
            tot["arr%d" % f] = len(topo.engines(T.cores[rank - 1], core))

    inc(Q.dma_start(T.pi8[0:8, :], T.par[:, :]), "par", 16)
    inc(Q.dma_start(T.bk[:, :], T.book[:, :]), "bookin", 16)

    inc(g.iota(T.ev[0:8, :], [[1, 8], [0, 16]], 0, -1, allow_small_or_imprecise_dtypes=True), "ka")
    inc(g.iota(T.kk[0:8, :], [[L, 16]], PAD, 0, allow_small_or_imprecise_dtypes=True), "ka")
    inc(g.iota(T.pn[:, 0:1], [[1, 1]], 0, 1), "ka")
    inc(g.iota(T.c16[:, :], [[16, 16]], 0, 0, allow_small_or_imprecise_dtypes=True), "ka")
    if not first:
        inc(g.iota(T.idv[:, :], [[-1, 128]], 0, 1, allow_small_or_imprecise_dtypes=True), "kb")
    inc(V.memset(T.win[:, 0:PAD], 0.0), "pad")
    if not first:
        inc(V.memset(T.low[:, 0:PAD], 0.0), "pad")
    wait(V, "ka")
    inc(V.tensor_scalar(T.pm[:, 0:1], T.pn[:, 0:1], 15, None, A.bitwise_and), "vs")
    inc(V.tensor_scalar(T.em[0:8, :], T.ev[0:8, :], 0.0, None, A.is_equal), "vs")
    inc(V.tensor_scalar(T.kf[0:8, :], T.kk[0:8, :], 15.5 / 32, None, A.add), "vs")
    wait(V, "vs")
    inc(V.tensor_copy(T.pmf[:, 0:1], T.pm[:, 0:1]), "vs")
    wait(V, "vs")
    inc(V.tensor_scalar(T.i16[:, :], T.c16[:, :], T.pmf[:, 0:1], None, A.add), "vs")
    if not first:
        wait(V, "kb")
        inc(V.tensor_scalar(T.ident[:, :], T.idv[:, :], 0.0, None, A.is_equal), "vid")

    wait(V, "par")
    inc(V.tensor_scalar(T.pf8[0:8, 0:16], T.pi8[0:8, 0:16], float(L), None, A.mult), "vs")
    ncol = 48 if first else 80
    for c0 in range(16, ncol, 32):
        inc(V.tensor_tensor(T.pf8[0:8, c0:c0 + 16], T.kf[0:8, :], T.pi8[0:8, c0:c0 + 16], A.subtract), "vs")
        inc(V.tensor_scalar(T.pf8[0:8, c0 + 16:c0 + 32], T.pi8[0:8, c0 + 16:c0 + 32], -1.0 / 32, 1.0, A.mult, A.add), "vs")
    wait(PE, "vs")
    inc(PE.matmul(T.ps[:, 0:ncol], T.em[0:8, :], T.pf8[0:8, 0:ncol], True, True), "pb")
    wait(V, "vs")
    wait(V, "pb")

    def word_list(f):
        inc(V.tensor_scalar(lst(T.offb, f), T.i16[:, :], T.ps[:, f:f + 1], None, A.add), "wl")

    def place_list(buf, c0, f, sem):
        inc(V.tensor_scalar(lst(buf, f), T.i16[:, :], T.ps[:, c0 + 16 + f:c0 + 17 + f], T.ps[:, c0 + f:c0 + f + 1],
                            A.mult, A.add), sem)

    def own_list(f):
        place_list(T.offo, 16, f, "ol")

    def own(f, a=0, b=L):
        return T.win[:, 0:PAD + L * f].indirect(lst(T.offo, f, a, b))

    def lower(f, a=0, b=L):
        return T.low[:, 0:PAD + L * (f + 1)].indirect(lst(T.offl, f, a, b))

    def words(q, out, offs, sem):
        src = T.bk[:, :].indirect(offs)
        if q is V:
            inc(V.tensor_scalar(out, src, sgn, None, A.mult), sem)
        else:
            inc(S.activation(out, src, Fn.Copy, scale=sgn), sem)

    def word_run(q, f0, f1):
        words(q, frs(T.bg, f0, f1), T.offb[:, 16 * f0:16 * (f1 + 1)], "bg%d" % f0)

    def clip(f, a, b, n, wide=False):
        out = fr(T.yf, f, a, b) if wide else fr(T.win, f, a, b, PAD)
        inc(V.tensor_scalar(out, fr(T.us, f, a, b), -127.0, 127.0, A.max, A.min), "cc", n)

    plan = store_plan(rank)
    batch_of = {}
    for j, (f0, f1, late) in enumerate(plan):
        for f in range(f0, f1 + 1):
            batch_of[f] = j

    def convert(q, f0, f1):
        sem = "cv%d" % batch_of[f0]
        src = T.win[:, PAD + L * f0:PAD + L * (f1 + 1)]
        wait(q, "cc", 2 * (f1 + 1))
        if q is V:
            inc(V.tensor_scalar(frs(T.yf, f0, f1), src, sgn, None, A.mult), sem)
        else:
            inc(S.activation(frs(T.yf, f0, f1), src, Fn.Copy, scale=sgn), sem)

    if first:
        for f in range(4):
            word_list(f)
        for f in range(1, 3):
            own_list(f)
        for q, (a, b) in zip((V, S), HALVES):
            wait(q, "wl", 2)
            wait(q, "bookin")
            words(q, fr(T.win, 0, a, b, PAD), lst(T.offb, 0, a, b), "cc")
            words(q, fr(T.bg, 1, a, b), lst(T.offb, 1, a, b), "bg1")
        wait(V, "pad")
        for f in range(2, F):
            wait(S, "wl", f + 1)
            word_run(S, f, f)
        for f in range(1, F):
            wait(V, "ol", f)
            wait(V, "bg%d" % f)
            wait(V, "cc", 2 * f)
            inc(V.tensor_tensor(fr(T.us, f), own(f), fr(T.bg, f), A.add), "a0")
            if f + 2 < F:
                own_list(f + 2)
            wait(V, "a0")
            clip(f, 0, L, 2)
            if f + 3 < F:
                word_list(f + 3)
        for f0 in range(0, F, 4):
            convert(S, f0, f0 + 3)
    else:
        for f in range(F):
            word_list(f)
        for f in range(F):
            place_list(T.offl, 48, f, "ll")
        for f in range(1, F):
            own_list(f)

        for q in (V, S):
            wait(q, "wl")
            wait(q, "bookin")
        word_run(V, F - 1 if rank == 1 else 12, F - 1)
        for f0, f1 in [(0, 1), (2, 5)] + ([] if rank == 1 else [(6, 11)]):
            word_run(S, f0, f1)
        between = dict(zip((1, 2, 4, 5, 7, 8, 10, 11, 12), range(6, 15)))

        wait(S, "ll")
        wait(S, "pad")
        wait(S, "arr0")
        for f in range(1, F):
            wait(S, "arr%d" % f)
            for a, b in HALVES:
                inc(S.activation(fr(T.lg, f, a, b), lower(f, a, b), Fn.Copy), "lg")
            if rank == 1:
                if f in between:
                    word_run(S, between[f], between[f])
            elif f >= 2:
                convert(S, f - 2, f - 2)
        if last:
            for h, (a, b) in enumerate(HALVES):
                wait(S, "cc", 2 * F - 3 + h)
                inc(S.activation(fr(T.yf, F - 2, a, b), fr(T.win, F - 2, a, b, PAD), Fn.Copy), "cv%d" % batch_of[F - 2])
        elif rank > 1:
            for f in range(F - 2, F):
                convert(S, f, f)

        for name in ("vid", "wl", "ll", "ol"):
            wait(PE, name)
        def psw(f, a=0, b=L):
            return fr(T.ps, 2 * (f % 8) + 1 - f // 8, a, b)

        wait(PE, "bg0")
        for f in range(1, F):
            if "bg%d" % f in tot:
                wait(PE, "bg%d" % f)
            if f > 8:
                wait(PE, "t0", f - 8)
                wait(PE, "t1", f - 8)
            inc(PE.matmul(psw(f), T.ident[:, :], fr(T.bg, f), True, True), "pe")

        def add(f, h):
            a, b = HALVES[h]
            if h == 0:
                wait(V, "pe", f)
            wait(V, "lg", 2 * (f - 1) + h + 1)
            inc(V.tensor_tensor(fr(T.cs, f, a, b), fr(T.lg, f, a, b), psw(f, a, b), A.add), "t%d" % h)

        for name in ("ll", "ol", "pad", "bg0", "arr0"):
            wait(V, name)
        for h, (a, b) in enumerate(HALVES):
            inc(V.tensor_tensor(fr(T.us, 0, a, b), lower(0, a, b), fr(T.bg, 0, a, b), A.add), "a%d" % h)
        for h, (a, b) in enumerate(HALVES):
            wait(V, "a%d" % h)
            clip(0, a, b, 1)
        add(1, 0)
        add(1, 1)
        for f in range(1, F):
            wait(V, "cc", 2 * f)
            for h, (a, b) in enumerate(HALVES):
                wait(V, "t%d" % h)
                inc(V.tensor_tensor(fr(T.us, f, a, b), own(f, a, b), fr(T.cs, f, a, b), A.add), "a%d" % h)
            for h, (a, b) in enumerate(HALVES):
                if h == 1 and f + 1 < F:
                    add(f + 1, 0)
                wait(V, "a%d" % h)
                clip(f, a, b, 1, last and f == F - 1)
            if f + 1 < F:
                add(f + 1, 1)
        if rank == 1:
            for f0 in range(0, F, 4):
                convert(V, f0, f0 + 1)
                convert(S, f0 + 2, f0 + 3)

    if not last:
        dst = T.cores[rank + 1]
        rid, pid, _ = topo.addr(dst)
        tot["sent"] = 0
        es = topo.engines(core, dst)
        pieces = [(0, a, b, 2 if first else h + 1, es[h::2]) for h, (a, b) in enumerate(HALVES)]
        for f, a, b, done, use in pieces + [(f, 0, L, 2 * (f + 1), es) for f in range(1, F)]:
            wait(g, "cc", done)
            g.remote_dma(fr(T.low, f, a, b, PAD), fr(T.win, f, a, b, PAD), T.sem["arr%d" % f], T.sem["sent"], pid, rid,
                         sum(1 << e for e in use))
            tot["sent"] += len(use)

    for j, (f0, f1, late) in enumerate(plan):
        wait(Q, "cv%d" % j)
        if late:
            wait(Q, "sent")
        c0, c1 = L * f0, L * (f1 + 1)
        if rank == NR - 2:
            c0, c1 = 192 * j, S_ALL if late else 192 * (j + 1)
        inc(Q.dma_start(T.y[:, c0:c1], T.yf[:, c0:c1]), "st", 16)
    if last:
        for h, q in enumerate((Q, S)):
            wait(q, "cc", 2 * F - 1 + h)
            inc(q.dma_start(fr(T.y, F - 1, H * h, H * (h + 1)), fr(T.yf, F - 1, H * h, H * (h + 1))), "st", 16)
    for name in tot:
        if name != "st" and seen.get(name, 0) < tot[name]:
            wait(g, name)
    wait(Q, "st")
